import numpy as np
import ml_dtypes


def mxq(x, axis, fmt="e4m3"):
    dtype, down = {"e4m3": (ml_dtypes.float8_e4m3fn, 7), "e5m2": (ml_dtypes.float8_e5m2, 14)}[fmt]
    v = np.moveaxis(np.asarray(x, np.float32).astype(ml_dtypes.bfloat16).astype(np.float64), axis, -1)
    blocks = v.reshape(v.shape[:-1] + (-1, 32))
    amax = np.abs(blocks).max(-1, keepdims=True)
    byte = np.maximum(np.where(amax > 0, np.frexp(amax)[1] - 1 + 127, 0) - down, 1)
    scale = np.exp2(byte - 127.0)
    codes = (blocks / scale).astype(np.float32).astype(dtype).astype(np.float64)
    return np.moveaxis((codes * scale).reshape(v.shape), -1, axis)


WIDE = False


def mx_kscale(k):
    if not WIDE:
        return np.ones(k)
    levels = np.array([10, -10, 5, -5, 0])
    if k % 512:
        return np.exp2(np.random.permutation(np.resize(levels, k // 32))).repeat(32)
    a = np.empty((k // 512, 16))
    for p in range(k // 512):
        a[p, :8] = np.random.permutation(np.resize(levels, 8))
        for g in range(8):
            far = levels[np.abs(levels - a[p, g]) >= 10]
            a[p, g + 8] = far[np.random.randint(len(far))]
    return np.exp2(a.ravel()).repeat(32)


def f64(x):
    return np.asarray(x).astype(np.float64)


def striped(idx):
    return np.tile(idx.reshape(-1, 16).T, (8, 1)).astype(np.uint16)


def unstriped(offs):
    return offs[:16].T.reshape(-1).astype(np.int64)


def pack_weight(w):
    k, n = w.shape
    w = f64(np.asarray(w, np.float32).astype(ml_dtypes.bfloat16)).reshape(k // 32, 32, n)
    amax = np.abs(w).max(1)
    byte = np.clip(np.where(amax > 0, np.frexp(amax)[1] - 1 + 127 - 7, 1), 1, 254)
    scaled = (w * np.exp2(127.0 - byte)[:, None, :]).reshape(k, n).astype(np.float32)
    words = np.ascontiguousarray(scaled.reshape(k // 512, 128, 4, n).transpose(0, 1, 3, 2)).astype(ml_dtypes.float8_e4m3fn).view(np.uint8)
    return words, np.ascontiguousarray(byte.astype(np.uint8).reshape(k // 512, 16, n))


def unpack_weight(words, scales):
    g, p, n, _ = words.shape
    vals = np.ascontiguousarray(words).view(ml_dtypes.float8_e4m3fn).astype(np.float64) * np.repeat(np.exp2(scales.astype(np.float64) - 127.0), 8, axis=1)[..., None]
    return vals.transpose(0, 1, 3, 2).reshape(g * 512, n)


K, T, S, D, N, V = 512, 2048, 1024, 4, 128, 256
P = 2 ** 7


def setup_inputs():
    n = np.random.standard_normal
    s = mx_kscale(K)[:, None]
    packed_xT = pack_weight(n((K, T)) * s)
    return {
        "x_words": packed_xT[0],
        "x_scales": packed_xT[1],
        "w1": (n((K, N)) / np.sqrt(K) / s).astype(np.float32),
        "dens": (np.tile(np.random.uniform(0.7, 1.4, V), (P, 1))).astype(np.float32),
        "offs": striped(np.random.permutation(T)[:S]),
        "nbr": striped(np.random.permutation(np.concatenate([np.arange(V), np.random.randint(0, V, S - V)]))),
    }


def reference(x_words, x_scales, w1, dens, offs, nbr):
    xq = unpack_weight(x_words, x_scales)[:, unstriped(offs)]
    y = mxq(f64(w1), 0, "e4m3").T @ xq
    dist = np.sqrt((y) ** 2 + 0.1)
    kdist = dist.reshape(len(dist), -1, D).max(axis=2)
    reach = np.maximum(kdist[:, unstriped(nbr)], dist)
    lrd = f64(dens)[:1] / (reach.reshape(len(reach), -1, D).mean(axis=2))
    gl = lrd[:, unstriped(nbr)]
    return np.log(gl.reshape(len(gl), -1, D).mean(axis=2)) - np.log(lrd) + 0.3 * kdist

@@ -1,0 +1,130 @@
+from contextlib import ExitStack
+
+import concourse.mybir as mybir
+
+F32 = mybir.dt.float32
+BF16 = mybir.dt.bfloat16
+I32 = mybir.dt.int32
+U32 = mybir.dt.uint32
+U16 = mybir.dt.uint16
+U8 = mybir.dt.uint8
+FP8X4 = mybir.dt.float8_e4m3fn_x4
+ALU = mybir.AluOpType
+ACT = mybir.ActivationFunctionType
+AXIS_X = mybir.AxisListType.X
+
+P = 128
+K, T, S, D, N, V = 512, 2048, 1024, 4, 128, 256
+PACK = 4
+STRIPE = 16
+SPARE = 144
+PRODUCT_PIECE = 256
+REACH_PIECES = (384, 384, 256)
+MEAN_PIECES = (384, 384, 256)
+FLOPS = 2 * K * N * S
+
+
+def spans(widths):
+    start = 0
+    found = []
+    for width in widths:
+        found.append((start, start + width))
+        start = start + width
+    return found
+
+
+def tile_picked_ylofx_log_p_kernel(tc, x_words, x_scales, w1, dens, offs, nbr, out):
+    nc = tc.nc
+    with ExitStack() as ctx:
+        sb = ctx.enter_context(tc.tile_pool(name="sb", bufs=1))
+        psum = ctx.enter_context(tc.psum_pool(name="psum", bufs=1))
+
+        offs_sb = sb.tile([P, S // STRIPE], U16, name="offs_sb")
+        nbr_sb = sb.tile([P, S // STRIPE], U16, name="nbr_sb")
+        scale_table = sb.tile([P, T], U8, name="scale_table", align_bytes=64)
+        word_table = sb.tile([P, T], U32, name="word_table", align_bytes=64)
+        w_raw = sb.tile([P, PACK, N], F32, name="w_raw")
+        dens_sb = sb.tile([P, V], F32, name="dens_sb")
+        ones = sb.tile([P, SPARE], F32, name="ones")
+        kdist = sb.tile([P, V + SPARE], F32, name="kdist")
+        lrd = sb.tile([P, V + SPARE], F32, name="lrd")
+
+        nc.vector.memset(scale_table[:].bitcast(I32), 0)
+        nc.vector.memset(ones[:], 1.0)
+
+        nc.sync.dma_start(offs_sb[:], offs)
+        nc.sync.dma_start(w_raw[:], w1.rearrange("(p j) n -> p j n", j=PACK))
+        nc.sync.dma_start(nbr_sb[:], nbr)
+        scale_rows = x_scales[0].bitcast(I32)
+        for q in range(4):
+            (nc.sync, nc.scalar)[q % 2].dma_start(scale_table[32 * q : 32 * q + 4, :].bitcast(I32), scale_rows[4 * q : 4 * q + 4, :])
+        nc.sync.dma_start(word_table[:].bitcast(I32), x_words[0].rearrange("p n t -> p (n t)").bitcast(I32))
+        nc.sync.dma_start(dens_sb[:], dens)
+        nc.scalar.activation(kdist[:, V:], ones[:], ACT.Sqrt)
+
+        w_grouped = sb.tile([P, N, PACK], BF16, name="w_grouped", align_bytes=64)
+        nc.scalar.copy(w_grouped[:], w_raw[:].rearrange("p j n -> p n j"))
+        w_codes = sb.tile([P, N], U32, name="w_codes", align_bytes=64)
+        w_scales = sb.tile([P, N], U8, name="w_scales", align_bytes=64)
+        x_scale_picked = sb.tile([P, S], U8, name="x_scale_picked", align_bytes=64)
+        nc.vector.tensor_copy(x_scale_picked[:, : S // 2], scale_table[:].indirect(offs_sb[:, : S // STRIPE // 2]))
+        nc.vector.quantize_mx(out=w_codes[:].bitcast(FP8X4), scales=w_scales[:], in_=w_grouped[:].rearrange("p n j -> p (n j)"))
+        nc.vector.tensor_copy(x_scale_picked[:, S // 2 :], scale_table[:].indirect(offs_sb[:, S // STRIPE // 2 :]))
+
+        squares = sb.tile([P, S], F32, name="squares")
+        dist = sb.tile([P, S], F32, name="dist")
+        ksquare = sb.tile([P, V], F32, name="ksquare")
+        pieces = spans([PRODUCT_PIECE] * (S // PRODUCT_PIECE))
+        for c, (a, b) in enumerate(pieces):
+            picked = sb.tile([P, b - a], U32, name="picked%d" % c, align_bytes=64)
+            nc.vector.tensor_copy(picked[:], word_table[:].indirect(offs_sb[:, a // STRIPE : b // STRIPE]))
+            y = psum.tile([P, 512], F32, name="y%d" % c)
+            nc.tensor.matmul_mx(
+                out=y[:, : b - a],
+                lhsT=w_codes[:].bitcast(FP8X4),
+                lhsT_scale=w_scales[:],
+                rhs=picked[:].bitcast(FP8X4),
+                rhs_scale=x_scale_picked[:, a:b],
+                start=True,
+                stop=True,
+            )
+            nc.scalar.activation(squares[:, a:b], y[:, : b - a], ACT.Square)
+        for a, b in spans((512, 256, 256)):
+            nc.vector.tensor_reduce(ksquare[:, a // D : b // D], squares[:, a:b].rearrange("p (v d) -> p v d", d=D), AXIS_X, ALU.max)
+            nc.scalar.activation(kdist[:, a // D : b // D], ksquare[:, a // D : b // D], ACT.Sqrt, bias=0.1)
+        for a, b in pieces:
+            nc.scalar.activation(dist[:, a:b], squares[:, a:b], ACT.Sqrt, bias=0.1)
+        nc.scalar.activation(lrd[:, V:], dist[:, S - SPARE :], ACT.Abs_reciprocal_sqrt)
+
+        kdist_nbr = sb.tile([P, S], F32, name="kdist_nbr")
+        reach = sb.tile([P, S], F32, name="reach")
+        reach_sum = sb.tile([P, V], F32, name="reach_sum")
+        mean_square = sb.tile([P, V], F32, name="mean_square")
+        inverse_mean = sb.tile([P, V], F32, name="inverse_mean")
+        for a, b in spans(REACH_PIECES):
+            nc.vector.tensor_copy(kdist_nbr[:, a:b], kdist[:].indirect(nbr_sb[:, a // STRIPE : b // STRIPE]))
+        for a, b in spans(REACH_PIECES):
+            points = slice(a // D, b // D)
+            nc.vector.tensor_tensor(reach[:, a:b], kdist_nbr[:, a:b], dist[:, a:b], ALU.max)
+            nc.vector.tensor_reduce(reach_sum[:, points], reach[:, a:b].rearrange("p (v d) -> p v d", d=D), AXIS_X, ALU.add)
+            nc.scalar.activation(mean_square[:, points], reach_sum[:, points], ACT.Square, scale=1.0 / D)
+            nc.scalar.activation(inverse_mean[:, points], mean_square[:, points], ACT.Abs_reciprocal_sqrt)
+            nc.vector.tensor_tensor(lrd[:, points], inverse_mean[:, points], dens_sb[:, points], ALU.mult)
+
+        log_lrd = sb.tile([P, V], F32, name="log_lrd")
+        own_term = sb.tile([P, V], F32, name="own_term")
+        lrd_nbr = sb.tile([P, S], F32, name="lrd_nbr")
+        lrd_sum = sb.tile([P, V], F32, name="lrd_sum")
+        log_mean = sb.tile([P, V], F32, name="log_mean")
+        result = sb.tile([P, V], F32, name="result")
+        for a, b in spans(MEAN_PIECES):
+            nc.vector.tensor_copy(lrd_nbr[:, a:b], lrd[:].indirect(nbr_sb[:, a // STRIPE : b // STRIPE]))
+        nc.scalar.activation(log_lrd[:], lrd[:, :V], ACT.Ln)
+        for a, b in spans(MEAN_PIECES):
+            points = slice(a // D, b // D)
+            nc.vector.tensor_reduce(lrd_sum[:, points], lrd_nbr[:, a:b].rearrange("p (v d) -> p v d", d=D), AXIS_X, ALU.add)
+            nc.scalar.activation(log_mean[:, points], lrd_sum[:, points], ACT.Ln, scale=1.0 / D)
+        nc.vector.scalar_tensor_tensor(own_term[:], kdist[:, :V], 0.3, log_lrd[:], ALU.mult, ALU.subtract)
+        for half in (slice(0, 192), slice(192, V)):
+            nc.vector.tensor_tensor(result[:, half], log_mean[:, half], own_term[:, half], ALU.add)
+            nc.sync.dma_start(out[:, half], result[:, half])

@@ -17,10 +17,17 @@ P = 128
 K, T, S, D, N, V = 512, 2048, 1024, 4, 128, 256
 PACK = 4
 STRIPE = 16
-SPARE = 144
+SPARE = 272
+WARM = 8
+EARLY = 256
 PRODUCT_PIECE = 256
-REACH_PIECES = (384, 384, 256)
-MEAN_PIECES = (384, 384, 256)
+MATMUL_PIECES = (256, 256, 256, 128, 128)
+KMAX_PIECES = (256, 256, 256, 128, 128)
+REACH_PIECES = (512, 384, 128)
+DENSITY_PIECES = (128, 128)
+MEAN_PIECES = (512, 384, 128)
+LOG_PIECES = (128, 128)
+STORE_PIECES = (128, 128)
 FLOPS = 2 * K * N * S
 
 
@@ -45,86 +52,119 @@ def tile_picked_ylofx_log_p_kernel(tc, x_words, x_scales, w1, dens, offs, nbr, o
         word_table = sb.tile([P, T], U32, name="word_table", align_bytes=64)
         w_raw = sb.tile([P, PACK, N], F32, name="w_raw")
         dens_sb = sb.tile([P, V], F32, name="dens_sb")
-        ones = sb.tile([P, SPARE], F32, name="ones")
         kdist = sb.tile([P, V + SPARE], F32, name="kdist")
+        ksquare = sb.tile([P, V + S // 2], F32, name="ksquare")
         lrd = sb.tile([P, V + SPARE], F32, name="lrd")
 
-        nc.vector.memset(scale_table[:].bitcast(I32), 0)
-        nc.vector.memset(ones[:], 1.0)
+        zeroed = scale_table[:].bitcast(I32)
+        nc.vector.memset(zeroed[:, : T // 8], 0)
+        nc.gpsimd.memset(zeroed[:, T // 8 :], 0)
+        nc.vector.memset(ksquare[:, V + WARM :], 1.0)
+        nc.scalar.activation(ksquare[:, V : V + WARM], ksquare[:, V + WARM : V + 2 * WARM], ACT.Sqrt)
+        nc.vector.memset(kdist[:, V:], 1.0)
+        nc.vector.memset(lrd[:, V + WARM :], 1.0)
 
-        nc.sync.dma_start(offs_sb[:], offs)
         nc.sync.dma_start(w_raw[:], w1.rearrange("(p j) n -> p j n", j=PACK))
-        nc.sync.dma_start(nbr_sb[:], nbr)
+        nc.sync.dma_start(offs_sb[:], offs)
         scale_rows = x_scales[0].bitcast(I32)
-        for q in range(4):
-            (nc.sync, nc.scalar)[q % 2].dma_start(scale_table[32 * q : 32 * q + 4, :].bitcast(I32), scale_rows[4 * q : 4 * q + 4, :])
+        for r in range(4):
+            nc.sync.dma_start(scale_table[r:P:32, :].bitcast(I32), scale_rows[r:16:4, :])
         nc.sync.dma_start(word_table[:].bitcast(I32), x_words[0].rearrange("p n t -> p (n t)").bitcast(I32))
+        nc.sync.dma_start(nbr_sb[:], nbr)
         nc.sync.dma_start(dens_sb[:], dens)
-        nc.scalar.activation(kdist[:, V:], ones[:], ACT.Sqrt)
 
         w_grouped = sb.tile([P, N, PACK], BF16, name="w_grouped", align_bytes=64)
-        nc.scalar.copy(w_grouped[:], w_raw[:].rearrange("p j n -> p n j"))
+        nc.vector.tensor_copy(w_grouped[:], w_raw[:].rearrange("p j n -> p n j"))
         w_codes = sb.tile([P, N], U32, name="w_codes", align_bytes=64)
         w_scales = sb.tile([P, N], U8, name="w_scales", align_bytes=64)
-        x_scale_picked = sb.tile([P, S], U8, name="x_scale_picked", align_bytes=64)
-        nc.vector.tensor_copy(x_scale_picked[:, : S // 2], scale_table[:].indirect(offs_sb[:, : S // STRIPE // 2]))
         nc.vector.quantize_mx(out=w_codes[:].bitcast(FP8X4), scales=w_scales[:], in_=w_grouped[:].rearrange("p n j -> p (n j)"))
-        nc.vector.tensor_copy(x_scale_picked[:, S // 2 :], scale_table[:].indirect(offs_sb[:, S // STRIPE // 2 :]))
 
+        picked_scales = sb.tile([P, S], U8, name="picked_scales", align_bytes=64)
+        nc.vector.tensor_copy(picked_scales[:], scale_table[:].indirect(offs_sb[:]))
+
+        picked_words = sb.tile([P, S], U32, name="picked_words", align_bytes=64)
         squares = sb.tile([P, S], F32, name="squares")
-        dist = sb.tile([P, S], F32, name="dist")
-        ksquare = sb.tile([P, V], F32, name="ksquare")
-        pieces = spans([PRODUCT_PIECE] * (S // PRODUCT_PIECE))
-        for c, (a, b) in enumerate(pieces):
-            picked = sb.tile([P, b - a], U32, name="picked%d" % c, align_bytes=64)
-            nc.vector.tensor_copy(picked[:], word_table[:].indirect(offs_sb[:, a // STRIPE : b // STRIPE]))
+        dist_early = sb.tile([P, S // 2], F32, name="dist_early")
+        dist_late = ksquare[:, V:]
+        for a, b in spans([PRODUCT_PIECE] * (S // PRODUCT_PIECE)):
+            nc.vector.tensor_copy(picked_words[:, a:b], word_table[:].indirect(offs_sb[:, a // STRIPE : b // STRIPE]))
+        for c, (a, b) in enumerate(spans(MATMUL_PIECES)):
             y = psum.tile([P, 512], F32, name="y%d" % c)
             nc.tensor.matmul_mx(
                 out=y[:, : b - a],
                 lhsT=w_codes[:].bitcast(FP8X4),
                 lhsT_scale=w_scales[:],
-                rhs=picked[:].bitcast(FP8X4),
-                rhs_scale=x_scale_picked[:, a:b],
+                rhs=picked_words[:, a:b].bitcast(FP8X4),
+                rhs_scale=picked_scales[:, a:b],
                 start=True,
                 stop=True,
             )
             nc.scalar.activation(squares[:, a:b], y[:, : b - a], ACT.Square)
-        for a, b in spans((512, 256, 256)):
+        for a, b in spans(KMAX_PIECES):
             nc.vector.tensor_reduce(ksquare[:, a // D : b // D], squares[:, a:b].rearrange("p (v d) -> p v d", d=D), AXIS_X, ALU.max)
-            nc.scalar.activation(kdist[:, a // D : b // D], ksquare[:, a // D : b // D], ACT.Sqrt, bias=0.1)
-        for a, b in pieces:
-            nc.scalar.activation(dist[:, a:b], squares[:, a:b], ACT.Sqrt, bias=0.1)
-        nc.scalar.activation(lrd[:, V:], dist[:, S - SPARE :], ACT.Abs_reciprocal_sqrt)
+        nc.scalar.activation(kdist[:, :V], ksquare[:, :V], ACT.Sqrt, bias=0.1)
+        for a, b in ((0, 256), (256, 512)):
+            nc.scalar.activation(dist_early[:, a:b], squares[:, a:b], ACT.Sqrt, bias=0.1)
 
+        def group_sum(sums, values, pairs, a, b, tree):
+            if tree:
+                nc.vector.tensor_tensor(pairs[:, a // 2 : b // 2], values[:, a:b:2], values[:, a + 1 : b : 2], ALU.add)
+            else:
+                nc.vector.tensor_reduce(sums[:, a // D : b // D], values[:, a:b].rearrange("p (v d) -> p v d", d=D), AXIS_X, ALU.add)
+
+        def pair_sum(sums, pairs, a, b):
+            nc.vector.tensor_tensor(sums[:, a // D : b // D], pairs[:, a // 2 : b // 2 : 2], pairs[:, a // 2 + 1 : b // 2 : 2], ALU.add)
+
+        ksquare_nbr = sb.tile([P, EARLY], F32, name="ksquare_nbr")
         kdist_nbr = sb.tile([P, S], F32, name="kdist_nbr")
         reach = sb.tile([P, S], F32, name="reach")
+        reach_pairs = sb.tile([P, S // 2], F32, name="reach_pairs")
         reach_sum = sb.tile([P, V], F32, name="reach_sum")
         mean_square = sb.tile([P, V], F32, name="mean_square")
         inverse_mean = sb.tile([P, V], F32, name="inverse_mean")
-        for a, b in spans(REACH_PIECES):
+        nc.vector.tensor_copy(ksquare_nbr[:], ksquare[:].indirect(nbr_sb[:, : EARLY // STRIPE]))
+        nc.scalar.activation(kdist_nbr[:, :EARLY], ksquare_nbr[:], ACT.Sqrt, bias=0.1)
+        nc.scalar.activation(dist_late, squares[:, S // 2 :], ACT.Sqrt, bias=0.1)
+        for a, b in ((EARLY, 768), (768, S)):
             nc.vector.tensor_copy(kdist_nbr[:, a:b], kdist[:].indirect(nbr_sb[:, a // STRIPE : b // STRIPE]))
-        for a, b in spans(REACH_PIECES):
-            points = slice(a // D, b // D)
-            nc.vector.tensor_tensor(reach[:, a:b], kdist_nbr[:, a:b], dist[:, a:b], ALU.max)
-            nc.vector.tensor_reduce(reach_sum[:, points], reach[:, a:b].rearrange("p (v d) -> p v d", d=D), AXIS_X, ALU.add)
-            nc.scalar.activation(mean_square[:, points], reach_sum[:, points], ACT.Square, scale=1.0 / D)
-            nc.scalar.activation(inverse_mean[:, points], mean_square[:, points], ACT.Abs_reciprocal_sqrt)
-            nc.vector.tensor_tensor(lrd[:, points], inverse_mean[:, points], dens_sb[:, points], ALU.mult)
+        reach_spans = spans(REACH_PIECES)
+        count = len(reach_spans)
+        for step in range(count + 3):
+            if 0 <= step - 1 < count:
+                a, b = reach_spans[step - 1]
+                nc.vector.tensor_tensor(reach[:, a:b], kdist_nbr[:, a:b], dist_early[:] if a == 0 else dist_late[:, a - S // 2 : b - S // 2], ALU.max)
+            if 0 <= step - 3 < 2:
+                pair_sum(reach_sum, reach_pairs, *reach_spans[step - 3])
+            if 0 <= step - 2 < count:
+                group_sum(reach_sum, reach, reach_pairs, *reach_spans[step - 2], step - 2 < 2)
+        nc.scalar.activation(lrd[:, V : V + WARM], dist_late[:, :WARM], ACT.Abs_reciprocal_sqrt)
+        for a, b in spans(DENSITY_PIECES):
+            nc.scalar.activation(mean_square[:, a:b], reach_sum[:, a:b], ACT.Square, scale=1.0 / D)
+            nc.scalar.activation(inverse_mean[:, a:b], mean_square[:, a:b], ACT.Abs_reciprocal_sqrt)
+            nc.vector.tensor_tensor(lrd[:, a:b], inverse_mean[:, a:b], dens_sb[:, a:b], ALU.mult)
 
         log_lrd = sb.tile([P, V], F32, name="log_lrd")
         own_term = sb.tile([P, V], F32, name="own_term")
         lrd_nbr = sb.tile([P, S], F32, name="lrd_nbr")
+        lrd_pairs = sb.tile([P, S // 2], F32, name="lrd_pairs")
         lrd_sum = sb.tile([P, V], F32, name="lrd_sum")
         log_mean = sb.tile([P, V], F32, name="log_mean")
         result = sb.tile([P, V], F32, name="result")
-        for a, b in spans(MEAN_PIECES):
-            nc.vector.tensor_copy(lrd_nbr[:, a:b], lrd[:].indirect(nbr_sb[:, a // STRIPE : b // STRIPE]))
         nc.scalar.activation(log_lrd[:], lrd[:, :V], ACT.Ln)
-        for a, b in spans(MEAN_PIECES):
-            points = slice(a // D, b // D)
-            nc.vector.tensor_reduce(lrd_sum[:, points], lrd_nbr[:, a:b].rearrange("p (v d) -> p v d", d=D), AXIS_X, ALU.add)
-            nc.scalar.activation(log_mean[:, points], lrd_sum[:, points], ACT.Ln, scale=1.0 / D)
+        mean_spans = spans(MEAN_PIECES)
+        count = len(mean_spans)
+        for step in range(count + 2):
+            if step < count:
+                a, b = mean_spans[step]
+                nc.vector.tensor_copy(lrd_nbr[:, a:b], lrd[:].indirect(nbr_sb[:, a // STRIPE : b // STRIPE]))
+            if 0 <= step - 2 < 2:
+                pair_sum(lrd_sum, lrd_pairs, *mean_spans[step - 2])
+            if 0 <= step - 1 < count:
+                group_sum(lrd_sum, lrd_nbr, lrd_pairs, *mean_spans[step - 1], step - 1 < 2)
+        for a, b in spans(LOG_PIECES):
+            nc.scalar.activation(log_mean[:, a:b], lrd_sum[:, a:b], ACT.Ln, scale=1.0 / D)
         nc.vector.scalar_tensor_tensor(own_term[:], kdist[:, :V], 0.3, log_lrd[:], ALU.mult, ALU.subtract)
-        for half in (slice(0, 192), slice(192, V)):
-            nc.vector.tensor_tensor(result[:, half], log_mean[:, half], own_term[:, half], ALU.add)
-            nc.sync.dma_start(out[:, half], result[:, half])
+
+        for a, b in spans(STORE_PIECES):
+            nc.vector.tensor_tensor(result[:, a:b], log_mean[:, a:b], own_term[:, a:b], ALU.add)
+            nc.sync.dma_start(out[:, a:b], result[:, a:b])

@@ -16,32 +16,46 @@ AXIS_X = mybir.AxisListType.X
 P = 128
 K, T, S, D, N, V = 512, 2048, 1024, 4, 128, 256
 PACK = 4
+QUADRANT = 32
 STRIPE = 16
-SPARE = 272
-WARM = 8
-EARLY = 256
-PRODUCT_PIECE = 256
-MATMUL_PIECES = (256, 256, 256, 128, 128)
-KMAX_PIECES = (256, 256, 256, 128, 128)
-REACH_PIECES = (512, 384, 128)
-DENSITY_PIECES = (128, 128)
-MEAN_PIECES = (512, 384, 128)
-LOG_PIECES = (128, 128)
-STORE_PIECES = (128, 128)
+BANK = 512
+HALF = S // 2
+EPSILON = 0.1
+KDIST_WEIGHT = 0.3
 FLOPS = 2 * K * N * S
+
+SPARE = HALF + STRIPE - V
+FIRST_USE = 8
+
+WORD_PIECES = (256, 256, 256, 256)
+PRODUCT_PIECES = (256, 256, 256, 128, 128)
+EARLY = 256
+KDIST_PIECES = (EARLY, 512, 256)
+REACH_PIECES = (HALF, 256, 128, 128)
+DENSITY_PIECES = (128, 64, 64)
+MEAN_PIECES = (HALF, 384, 128)
+OUT_PIECES = (128, 128)
+PAIRED_PIECES = 2
 
 
 def spans(widths):
-    start = 0
-    found = []
-    for width in widths:
-        found.append((start, start + width))
-        start = start + width
-    return found
+    ends = [sum(widths[: i + 1]) for i in range(len(widths))]
+    return [(end - width, end) for width, end in zip(widths, ends)]
 
 
 def tile_picked_ylofx_log_p_kernel(tc, x_words, x_scales, w1, dens, offs, nbr, out):
     nc = tc.nc
+
+    def gather(dst, window, entries, first, end):
+        nc.vector.tensor_copy(dst, window[:].indirect(entries[:, first // STRIPE : end // STRIPE]))
+
+    def reduce_points(dst, values, first, end, op):
+        groups = values[:, first:end].rearrange("p (v d) -> p v d", d=D)
+        nc.vector.tensor_reduce(dst[:, first // D : end // D], groups, AXIS_X, op)
+
+    def add_pairs(engine, dst, values, first, end):
+        engine.tensor_tensor(dst[:, first // 2 : end // 2], values[:, first:end:2], values[:, first + 1 : end : 2], ALU.add)
+
     with ExitStack() as ctx:
         sb = ctx.enter_context(tc.tile_pool(name="sb", bufs=1))
         psum = ctx.enter_context(tc.psum_pool(name="psum", bufs=1))
@@ -53,22 +67,22 @@ def tile_picked_ylofx_log_p_kernel(tc, x_words, x_scales, w1, dens, offs, nbr, o
         w_raw = sb.tile([P, PACK, N], F32, name="w_raw")
         dens_sb = sb.tile([P, V], F32, name="dens_sb")
         kdist = sb.tile([P, V + SPARE], F32, name="kdist")
-        ksquare = sb.tile([P, V + S // 2], F32, name="ksquare")
+        ksquare = sb.tile([P, V + HALF], F32, name="ksquare")
         lrd = sb.tile([P, V + SPARE], F32, name="lrd")
 
-        zeroed = scale_table[:].bitcast(I32)
-        nc.vector.memset(zeroed[:, : T // 8], 0)
-        nc.gpsimd.memset(zeroed[:, T // 8 :], 0)
-        nc.vector.memset(ksquare[:, V + WARM :], 1.0)
-        nc.scalar.activation(ksquare[:, V : V + WARM], ksquare[:, V + WARM : V + 2 * WARM], ACT.Sqrt)
+        scale_table_words = scale_table[:].bitcast(I32)
+        nc.vector.memset(scale_table_words[:, : T // 8], 0)
+        nc.gpsimd.memset(scale_table_words[:, T // 8 :], 0)
+        nc.vector.memset(ksquare[:, V + FIRST_USE :], 1.0)
+        nc.scalar.activation(ksquare[:, V : V + FIRST_USE], ksquare[:, V + FIRST_USE : V + 2 * FIRST_USE], ACT.Sqrt)
         nc.vector.memset(kdist[:, V:], 1.0)
-        nc.vector.memset(lrd[:, V + WARM :], 1.0)
+        nc.vector.memset(lrd[:, V + FIRST_USE :], 1.0)
 
         nc.sync.dma_start(w_raw[:], w1.rearrange("(p j) n -> p j n", j=PACK))
         nc.sync.dma_start(offs_sb[:], offs)
         scale_rows = x_scales[0].bitcast(I32)
         for r in range(4):
-            nc.sync.dma_start(scale_table[r:P:32, :].bitcast(I32), scale_rows[r:16:4, :])
+            nc.sync.dma_start(scale_table[r:P:QUADRANT, :].bitcast(I32), scale_rows[r : K // 32 : 4, :])
         nc.sync.dma_start(word_table[:].bitcast(I32), x_words[0].rearrange("p n t -> p (n t)").bitcast(I32))
         nc.sync.dma_start(nbr_sb[:], nbr)
         nc.sync.dma_start(dens_sb[:], dens)
@@ -80,16 +94,14 @@ def tile_picked_ylofx_log_p_kernel(tc, x_words, x_scales, w1, dens, offs, nbr, o
         nc.vector.quantize_mx(out=w_codes[:].bitcast(FP8X4), scales=w_scales[:], in_=w_grouped[:].rearrange("p n j -> p (n j)"))
 
         picked_scales = sb.tile([P, S], U8, name="picked_scales", align_bytes=64)
-        nc.vector.tensor_copy(picked_scales[:], scale_table[:].indirect(offs_sb[:]))
-
+        gather(picked_scales[:], scale_table, offs_sb, 0, S)
         picked_words = sb.tile([P, S], U32, name="picked_words", align_bytes=64)
+        for a, b in spans(WORD_PIECES):
+            gather(picked_words[:, a:b], word_table, offs_sb, a, b)
+
         squares = sb.tile([P, S], F32, name="squares")
-        dist_early = sb.tile([P, S // 2], F32, name="dist_early")
-        dist_late = ksquare[:, V:]
-        for a, b in spans([PRODUCT_PIECE] * (S // PRODUCT_PIECE)):
-            nc.vector.tensor_copy(picked_words[:, a:b], word_table[:].indirect(offs_sb[:, a // STRIPE : b // STRIPE]))
-        for c, (a, b) in enumerate(spans(MATMUL_PIECES)):
-            y = psum.tile([P, 512], F32, name="y%d" % c)
+        for c, (a, b) in enumerate(spans(PRODUCT_PIECES)):
+            y = psum.tile([P, BANK], F32, name="y%d" % c)
             nc.tensor.matmul_mx(
                 out=y[:, : b - a],
                 lhsT=w_codes[:].bitcast(FP8X4),
@@ -100,71 +112,68 @@ def tile_picked_ylofx_log_p_kernel(tc, x_words, x_scales, w1, dens, offs, nbr, o
                 stop=True,
             )
             nc.scalar.activation(squares[:, a:b], y[:, : b - a], ACT.Square)
-        for a, b in spans(KMAX_PIECES):
-            nc.vector.tensor_reduce(ksquare[:, a // D : b // D], squares[:, a:b].rearrange("p (v d) -> p v d", d=D), AXIS_X, ALU.max)
-        nc.scalar.activation(kdist[:, :V], ksquare[:, :V], ACT.Sqrt, bias=0.1)
-        for a, b in ((0, 256), (256, 512)):
-            nc.scalar.activation(dist_early[:, a:b], squares[:, a:b], ACT.Sqrt, bias=0.1)
 
-        def group_sum(sums, values, pairs, a, b, tree):
-            if tree:
-                nc.vector.tensor_tensor(pairs[:, a // 2 : b // 2], values[:, a:b:2], values[:, a + 1 : b : 2], ALU.add)
-            else:
-                nc.vector.tensor_reduce(sums[:, a // D : b // D], values[:, a:b].rearrange("p (v d) -> p v d", d=D), AXIS_X, ALU.add)
+        for a, b in spans(PRODUCT_PIECES):
+            reduce_points(ksquare, squares, a, b, ALU.max)
+        nc.scalar.activation(kdist[:, :V], ksquare[:, :V], ACT.Sqrt, bias=EPSILON)
+        dist_early = sb.tile([P, HALF], F32, name="dist_early")
+        for a, b in spans((HALF // 2, HALF // 2)):
+            nc.scalar.activation(dist_early[:, a:b], squares[:, a:b], ACT.Sqrt, bias=EPSILON)
 
-        def pair_sum(sums, pairs, a, b):
-            nc.vector.tensor_tensor(sums[:, a // D : b // D], pairs[:, a // 2 : b // 2 : 2], pairs[:, a // 2 + 1 : b // 2 : 2], ALU.add)
-
-        ksquare_nbr = sb.tile([P, EARLY], F32, name="ksquare_nbr")
         kdist_nbr = sb.tile([P, S], F32, name="kdist_nbr")
+        ksquare_nbr = sb.tile([P, EARLY], F32, name="ksquare_nbr")
+        gather(ksquare_nbr[:], ksquare, nbr_sb, 0, EARLY)
+        nc.scalar.activation(kdist_nbr[:, :EARLY], ksquare_nbr[:], ACT.Sqrt, bias=EPSILON)
+        dist_late = ksquare[:, V:]
+        nc.scalar.activation(dist_late, squares[:, HALF:], ACT.Sqrt, bias=EPSILON)
+        for a, b in spans(KDIST_PIECES)[1:]:
+            gather(kdist_nbr[:, a:b], kdist, nbr_sb, a, b)
+
         reach = sb.tile([P, S], F32, name="reach")
-        reach_pairs = sb.tile([P, S // 2], F32, name="reach_pairs")
+        reach_pairs = sb.tile([P, HALF], F32, name="reach_pairs")
         reach_sum = sb.tile([P, V], F32, name="reach_sum")
+        reach_spans = spans(REACH_PIECES)
+        for step in range(len(reach_spans) + 1):
+            if step < len(reach_spans):
+                a, b = reach_spans[step]
+                dist = dist_early[:, a:b] if b <= HALF else dist_late[:, a - HALF : b - HALF]
+                nc.vector.tensor_tensor(reach[:, a:b], kdist_nbr[:, a:b], dist, ALU.max)
+            if 0 <= step - 2 < PAIRED_PIECES:
+                a, b = reach_spans[step - 2]
+                add_pairs(nc.vector, reach_sum, reach_pairs, a // 2, b // 2)
+            if 0 <= step - 1 < PAIRED_PIECES:
+                add_pairs(nc.vector, reach_pairs, reach, *reach_spans[step - 1])
+            elif step >= 1:
+                reduce_points(reach_sum, reach, *reach_spans[step - 1], ALU.add)
+
         mean_square = sb.tile([P, V], F32, name="mean_square")
         inverse_mean = sb.tile([P, V], F32, name="inverse_mean")
-        nc.vector.tensor_copy(ksquare_nbr[:], ksquare[:].indirect(nbr_sb[:, : EARLY // STRIPE]))
-        nc.scalar.activation(kdist_nbr[:, :EARLY], ksquare_nbr[:], ACT.Sqrt, bias=0.1)
-        nc.scalar.activation(dist_late, squares[:, S // 2 :], ACT.Sqrt, bias=0.1)
-        for a, b in ((EARLY, 768), (768, S)):
-            nc.vector.tensor_copy(kdist_nbr[:, a:b], kdist[:].indirect(nbr_sb[:, a // STRIPE : b // STRIPE]))
-        reach_spans = spans(REACH_PIECES)
-        count = len(reach_spans)
-        for step in range(count + 3):
-            if 0 <= step - 1 < count:
-                a, b = reach_spans[step - 1]
-                nc.vector.tensor_tensor(reach[:, a:b], kdist_nbr[:, a:b], dist_early[:] if a == 0 else dist_late[:, a - S // 2 : b - S // 2], ALU.max)
-            if 0 <= step - 3 < 2:
-                pair_sum(reach_sum, reach_pairs, *reach_spans[step - 3])
-            if 0 <= step - 2 < count:
-                group_sum(reach_sum, reach, reach_pairs, *reach_spans[step - 2], step - 2 < 2)
-        nc.scalar.activation(lrd[:, V : V + WARM], dist_late[:, :WARM], ACT.Abs_reciprocal_sqrt)
+        nc.scalar.activation(lrd[:, V : V + FIRST_USE], dist_late[:, :FIRST_USE], ACT.Abs_reciprocal_sqrt)
         for a, b in spans(DENSITY_PIECES):
             nc.scalar.activation(mean_square[:, a:b], reach_sum[:, a:b], ACT.Square, scale=1.0 / D)
             nc.scalar.activation(inverse_mean[:, a:b], mean_square[:, a:b], ACT.Abs_reciprocal_sqrt)
             nc.vector.tensor_tensor(lrd[:, a:b], inverse_mean[:, a:b], dens_sb[:, a:b], ALU.mult)
 
         log_lrd = sb.tile([P, V], F32, name="log_lrd")
-        own_term = sb.tile([P, V], F32, name="own_term")
-        lrd_nbr = sb.tile([P, S], F32, name="lrd_nbr")
-        lrd_pairs = sb.tile([P, S // 2], F32, name="lrd_pairs")
-        lrd_sum = sb.tile([P, V], F32, name="lrd_sum")
-        log_mean = sb.tile([P, V], F32, name="log_mean")
-        result = sb.tile([P, V], F32, name="result")
         nc.scalar.activation(log_lrd[:], lrd[:, :V], ACT.Ln)
-        mean_spans = spans(MEAN_PIECES)
-        count = len(mean_spans)
-        for step in range(count + 2):
-            if step < count:
-                a, b = mean_spans[step]
-                nc.vector.tensor_copy(lrd_nbr[:, a:b], lrd[:].indirect(nbr_sb[:, a // STRIPE : b // STRIPE]))
-            if 0 <= step - 2 < 2:
-                pair_sum(lrd_sum, lrd_pairs, *mean_spans[step - 2])
-            if 0 <= step - 1 < count:
-                group_sum(lrd_sum, lrd_nbr, lrd_pairs, *mean_spans[step - 1], step - 1 < 2)
-        for a, b in spans(LOG_PIECES):
-            nc.scalar.activation(log_mean[:, a:b], lrd_sum[:, a:b], ACT.Ln, scale=1.0 / D)
-        nc.vector.scalar_tensor_tensor(own_term[:], kdist[:, :V], 0.3, log_lrd[:], ALU.mult, ALU.subtract)
 
-        for a, b in spans(STORE_PIECES):
+        lrd_nbr = sb.tile([P, S], F32, name="lrd_nbr")
+        lrd_pairs = sb.tile([P, HALF], F32, name="lrd_pairs")
+        lrd_sum = sb.tile([P, V], F32, name="lrd_sum")
+        mean_spans = spans(MEAN_PIECES)
+        for a, b in mean_spans:
+            gather(lrd_nbr[:, a:b], lrd, nbr_sb, a, b)
+        add_pairs(nc.gpsimd, lrd_pairs, lrd_nbr, 0, HALF)
+        add_pairs(nc.gpsimd, lrd_sum, lrd_pairs, 0, HALF // 2)
+        for a, b in mean_spans[1:]:
+            reduce_points(lrd_sum, lrd_nbr, a, b, ALU.add)
+
+        log_mean = sb.tile([P, V], F32, name="log_mean")
+        own_term = sb.tile([P, V], F32, name="own_term")
+        result = sb.tile([P, V], F32, name="result")
+        for a, b in spans(OUT_PIECES):
+            nc.scalar.activation(log_mean[:, a:b], lrd_sum[:, a:b], ACT.Ln, scale=1.0 / D)
+        nc.vector.scalar_tensor_tensor(own_term[:], kdist[:, :V], KDIST_WEIGHT, log_lrd[:], ALU.mult, ALU.subtract)
+        for a, b in spans(OUT_PIECES):
             nc.vector.tensor_tensor(result[:, a:b], log_mean[:, a:b], own_term[:, a:b], ALU.add)
             nc.sync.dma_start(out[:, a:b], result[:, a:b])

from contextlib import ExitStack

import concourse.mybir as mybir

F32 = mybir.dt.float32
BF16 = mybir.dt.bfloat16
I32 = mybir.dt.int32
U32 = mybir.dt.uint32
U16 = mybir.dt.uint16
U8 = mybir.dt.uint8
FP8X4 = mybir.dt.float8_e4m3fn_x4
ALU = mybir.AluOpType
ACT = mybir.ActivationFunctionType
AXIS_X = mybir.AxisListType.X

P = 128
K, T, S, D, N, V = 512, 2048, 1024, 4, 128, 256
PACK = 4
QUADRANT = 32
STRIPE = 16
BANK = 512
HALF = S // 2
EPSILON = 0.1
KDIST_WEIGHT = 0.3
FLOPS = 2 * K * N * S

SPARE = HALF + STRIPE - V
FIRST_USE = 8

WORD_PIECES = (256, 256, 256, 256)
PRODUCT_PIECES = (256, 256, 256, 128, 128)
EARLY = 256
KDIST_PIECES = (EARLY, 512, 256)
REACH_PIECES = (HALF, 256, 128, 128)
DENSITY_PIECES = (128, 64, 64)
MEAN_PIECES = (HALF, 384, 128)
OUT_PIECES = (128, 128)
PAIRED_PIECES = 2


def spans(widths):
    ends = [sum(widths[: i + 1]) for i in range(len(widths))]
    return [(end - width, end) for width, end in zip(widths, ends)]


def tile_picked_ylofx_log_p_kernel(tc, x_words, x_scales, w1, dens, offs, nbr, out):
    nc = tc.nc

    def gather(dst, window, entries, first, end):
        nc.vector.tensor_copy(dst, window[:].indirect(entries[:, first // STRIPE : end // STRIPE]))

    def reduce_points(dst, values, first, end, op):
        groups = values[:, first:end].rearrange("p (v d) -> p v d", d=D)
        nc.vector.tensor_reduce(dst[:, first // D : end // D], groups, AXIS_X, op)

    def add_pairs(engine, dst, values, first, end):
        engine.tensor_tensor(dst[:, first // 2 : end // 2], values[:, first:end:2], values[:, first + 1 : end : 2], ALU.add)

    with ExitStack() as ctx:
        sb = ctx.enter_context(tc.tile_pool(name="sb", bufs=1))
        psum = ctx.enter_context(tc.psum_pool(name="psum", bufs=1))

        offs_sb = sb.tile([P, S // STRIPE], U16, name="offs_sb")
        nbr_sb = sb.tile([P, S // STRIPE], U16, name="nbr_sb")
        scale_table = sb.tile([P, T], U8, name="scale_table", align_bytes=64)
        word_table = sb.tile([P, T], U32, name="word_table", align_bytes=64)
        w_raw = sb.tile([P, PACK, N], F32, name="w_raw")
        dens_sb = sb.tile([P, V], F32, name="dens_sb")
        kdist = sb.tile([P, V + SPARE], F32, name="kdist")
        ksquare = sb.tile([P, V + HALF], F32, name="ksquare")
        lrd = sb.tile([P, V + SPARE], F32, name="lrd")

        scale_table_words = scale_table[:].bitcast(I32)
        nc.vector.memset(scale_table_words[:, : T // 8], 0)
        nc.gpsimd.memset(scale_table_words[:, T // 8 :], 0)
        nc.vector.memset(ksquare[:, V + FIRST_USE :], 1.0)
        nc.scalar.activation(ksquare[:, V : V + FIRST_USE], ksquare[:, V + FIRST_USE : V + 2 * FIRST_USE], ACT.Sqrt)
        nc.vector.memset(kdist[:, V:], 1.0)
        nc.vector.memset(lrd[:, V + FIRST_USE :], 1.0)

        nc.sync.dma_start(w_raw[:], w1.rearrange("(p j) n -> p j n", j=PACK))
        nc.sync.dma_start(offs_sb[:], offs)
        scale_rows = x_scales[0].bitcast(I32)
        for r in range(4):
            nc.sync.dma_start(scale_table[r:P:QUADRANT, :].bitcast(I32), scale_rows[r : K // 32 : 4, :])
        nc.sync.dma_start(word_table[:].bitcast(I32), x_words[0].rearrange("p n t -> p (n t)").bitcast(I32))
        nc.sync.dma_start(nbr_sb[:], nbr)
        nc.sync.dma_start(dens_sb[:], dens)

        w_grouped = sb.tile([P, N, PACK], BF16, name="w_grouped", align_bytes=64)
        nc.vector.tensor_copy(w_grouped[:], w_raw[:].rearrange("p j n -> p n j"))
        w_codes = sb.tile([P, N], U32, name="w_codes", align_bytes=64)
        w_scales = sb.tile([P, N], U8, name="w_scales", align_bytes=64)
        nc.vector.quantize_mx(out=w_codes[:].bitcast(FP8X4), scales=w_scales[:], in_=w_grouped[:].rearrange("p n j -> p (n j)"))

        picked_scales = sb.tile([P, S], U8, name="picked_scales", align_bytes=64)
        gather(picked_scales[:], scale_table, offs_sb, 0, S)
        picked_words = sb.tile([P, S], U32, name="picked_words", align_bytes=64)
        for a, b in spans(WORD_PIECES):
            gather(picked_words[:, a:b], word_table, offs_sb, a, b)

        squares = sb.tile([P, S], F32, name="squares")
        for c, (a, b) in enumerate(spans(PRODUCT_PIECES)):
            y = psum.tile([P, BANK], F32, name="y%d" % c)
            nc.tensor.matmul_mx(
                out=y[:, : b - a],
                lhsT=w_codes[:].bitcast(FP8X4),
                lhsT_scale=w_scales[:],
                rhs=picked_words[:, a:b].bitcast(FP8X4),
                rhs_scale=picked_scales[:, a:b],
                start=True,
                stop=True,
            )
            nc.scalar.activation(squares[:, a:b], y[:, : b - a], ACT.Square)

        for a, b in spans(PRODUCT_PIECES):
            reduce_points(ksquare, squares, a, b, ALU.max)
        nc.scalar.activation(kdist[:, :V], ksquare[:, :V], ACT.Sqrt, bias=EPSILON)
        dist_early = sb.tile([P, HALF], F32, name="dist_early")
        for a, b in spans((HALF // 2, HALF // 2)):
            nc.scalar.activation(dist_early[:, a:b], squares[:, a:b], ACT.Sqrt, bias=EPSILON)

        kdist_nbr = sb.tile([P, S], F32, name="kdist_nbr")
        ksquare_nbr = sb.tile([P, EARLY], F32, name="ksquare_nbr")
        gather(ksquare_nbr[:], ksquare, nbr_sb, 0, EARLY)
        nc.scalar.activation(kdist_nbr[:, :EARLY], ksquare_nbr[:], ACT.Sqrt, bias=EPSILON)
        dist_late = ksquare[:, V:]
        nc.scalar.activation(dist_late, squares[:, HALF:], ACT.Sqrt, bias=EPSILON)
        for a, b in spans(KDIST_PIECES)[1:]:
            gather(kdist_nbr[:, a:b], kdist, nbr_sb, a, b)

        reach = sb.tile([P, S], F32, name="reach")
        reach_pairs = sb.tile([P, HALF], F32, name="reach_pairs")
        reach_sum = sb.tile([P, V], F32, name="reach_sum")
        reach_spans = spans(REACH_PIECES)
        for step in range(len(reach_spans) + 1):
            if step < len(reach_spans):
                a, b = reach_spans[step]
                dist = dist_early[:, a:b] if b <= HALF else dist_late[:, a - HALF : b - HALF]
                nc.vector.tensor_tensor(reach[:, a:b], kdist_nbr[:, a:b], dist, ALU.max)
            if 0 <= step - 2 < PAIRED_PIECES:
                a, b = reach_spans[step - 2]
                add_pairs(nc.vector, reach_sum, reach_pairs, a // 2, b // 2)
            if 0 <= step - 1 < PAIRED_PIECES:
                add_pairs(nc.vector, reach_pairs, reach, *reach_spans[step - 1])
            elif step >= 1:
                reduce_points(reach_sum, reach, *reach_spans[step - 1], ALU.add)

        mean_square = sb.tile([P, V], F32, name="mean_square")
        inverse_mean = sb.tile([P, V], F32, name="inverse_mean")
        nc.scalar.activation(lrd[:, V : V + FIRST_USE], dist_late[:, :FIRST_USE], ACT.Abs_reciprocal_sqrt)
        for a, b in spans(DENSITY_PIECES):
            nc.scalar.activation(mean_square[:, a:b], reach_sum[:, a:b], ACT.Square, scale=1.0 / D)
            nc.scalar.activation(inverse_mean[:, a:b], mean_square[:, a:b], ACT.Abs_reciprocal_sqrt)
            nc.vector.tensor_tensor(lrd[:, a:b], inverse_mean[:, a:b], dens_sb[:, a:b], ALU.mult)

        log_lrd = sb.tile([P, V], F32, name="log_lrd")
        nc.scalar.activation(log_lrd[:], lrd[:, :V], ACT.Ln)

        lrd_nbr = sb.tile([P, S], F32, name="lrd_nbr")
        lrd_pairs = sb.tile([P, HALF], F32, name="lrd_pairs")
        lrd_sum = sb.tile([P, V], F32, name="lrd_sum")
        mean_spans = spans(MEAN_PIECES)
        for a, b in mean_spans:
            gather(lrd_nbr[:, a:b], lrd, nbr_sb, a, b)
        add_pairs(nc.gpsimd, lrd_pairs, lrd_nbr, 0, HALF)
        add_pairs(nc.gpsimd, lrd_sum, lrd_pairs, 0, HALF // 2)
        for a, b in mean_spans[1:]:
            reduce_points(lrd_sum, lrd_nbr, a, b, ALU.add)

        log_mean = sb.tile([P, V], F32, name="log_mean")
        own_term = sb.tile([P, V], F32, name="own_term")
        result = sb.tile([P, V], F32, name="result")
        for a, b in spans(OUT_PIECES):
            nc.scalar.activation(log_mean[:, a:b], lrd_sum[:, a:b], ACT.Ln, scale=1.0 / D)
        nc.vector.scalar_tensor_tensor(own_term[:], kdist[:, :V], KDIST_WEIGHT, log_lrd[:], ALU.mult, ALU.subtract)
        for a, b in spans(OUT_PIECES):
            nc.vector.tensor_tensor(result[:, a:b], log_mean[:, a:b], own_term[:, a:b], ALU.add)
            nc.sync.dma_start(out[:, a:b], result[:, a:b])
